import numpy as np, ml_dtypes
CORES = [16,18,20,22]
N = 4
import mx_ref
BF = ml_dtypes.bfloat16
def gcols(t, e):
    v = np.concatenate([t.reshape(8, 16, -1, 4), np.zeros((8, 16, 1, 4), BF)], axis=2)
    return np.ascontiguousarray(np.stack([v[g][:, e[g]] for g in range(8)])).reshape(128, -1)
def tile(rs):
    return np.stack(rs, axis=2).reshape(128, -1).astype(BF)
def cut(t, i, w=512):
    return t[:, w * i:w * i + w]
def pick(q, e):
    c = np.concatenate([q[0].reshape(128, -1, 4), np.zeros((128, 1, 4), np.uint8)], axis=1); s = np.concatenate([q[1], np.ones((16, 1), np.uint8)], axis=1)
    return (np.ascontiguousarray(c[:, e].reshape(128, -1)), np.ascontiguousarray(s[:, e]))
def join(*qs):
    return (np.concatenate([q[0] for q in qs], axis=1), np.concatenate([q[1] for q in qs], axis=1))
def put(q, e, v):
    c, s = q[0].reshape(128, -1, 4).copy(), q[1].copy(); c[:, e] = v[0].reshape(128, -1, 4); s[:, e] = v[1]
    return (c.reshape(128, -1), s)
def pk(c, s):
    return (np.ascontiguousarray(c), mx_ref.live(s))
def emit(q):
    return q[0], q[1]
def packed(v, rng):
    q = [mx_ref.quantize(np.ascontiguousarray(v[r])) for r in range(N)]
    return np.stack([a for a, b in q]), np.stack([mx_ref.plane(b, rng) for a, b in q])
def values_of_codes():
    e, c = np.zeros((128, 128, 4), np.float32), np.zeros((128, 2, 4), np.uint8)
    e[np.arange(128), np.arange(128), 0] = 1
    c[:127, :, 0] = np.arange(256).reshape(2, 128).T[:127]
    return mx_ref.matmul(mx_ref.quantize(e.reshape(128, 512).astype(BF)), (c.reshape(128, 8), np.full((16, 2), 127, np.uint8))).T.reshape(-1).astype(np.float64)
CODE_VALUE, SCALE_VALUE = values_of_codes(), 2.0 ** (np.arange(256) - 127.0)
def decode(q):
    return (CODE_VALUE[q[0]].reshape(16, 8, -1, 4) * SCALE_VALUE[q[1]][:, None, :, None] + 0.0).reshape(128, -1).astype(np.float32)
def f(rng, *shape):
    return mx_ref.flush((rng.standard_normal(shape, dtype=np.float32) * np.exp2(rng.integers(-2, 3, shape[:-1] + (1,)))).astype(BF))
def wide(rng, *shape, cols=0):
    v = rng.standard_normal(shape, dtype=np.float32) * np.exp2(rng.integers(-12, 13, shape)).astype(np.float32)
    if cols: v *= np.repeat(np.exp2(rng.integers(-cols, cols + 1, shape[:-2] + (1, shape[-1] // 4))) * (rng.random(shape[:-2] + (1, shape[-1] // 4)) > 0.0625), 4, axis=-1).astype(np.float32)
    return mx_ref.flush(v.astype(BF))
C, K, M, S, H, R = 320, 128, 64, 5, 7, 3
STEP = [1, 3, 1]
def gap(p, q):
    return np.abs(p.reshape(8, M, 1, S) - q.reshape(8, 1, M, S))
def match(p, q, lag):
    back = (np.arange(C) - lag[:, None]) % C
    d = np.maximum(gap(p, q), gap(np.take_along_axis(p, back, 1), np.take_along_axis(q, back, 1)))
    m = (S * np.argmin(d, axis=2) + np.arange(S)).reshape(8, C)
    e = np.sort(np.argsort(np.min(d, axis=2).reshape(8, C), axis=1, kind="stable")[:, :K], axis=1)
    return e, np.take_along_axis(m, e, 1)
def gput(t, e, h):
    a, b = t.reshape(8, 16, -1, 4).copy(), h.reshape(8, 16, -1, 4)
    for g in range(8): a[g][:, e[g]] = b[g]
    return a.reshape(128, -1)
def big(v):
    v = v.astype(np.float32)
    v[np.abs(v) < np.float32(2.0 ** -16)] = 0
    return v.astype(BF)
def numbers_of(rng):
    return {"x": big(f(rng, N, 128, 4 * C)), "u": np.array(f(rng, N, 128, 512)), "v": np.array(f(rng, N, 128, 512))}
def weights(rng, still=[]):
    w = big(f(rng, N, 128, 2048)).reshape(N, 8, 16, 4, 8, 16, 4)
    for i in still:
        w[:, :, i] = 0
        w[:, :, :, :, :, i] = 0
    c, p = packed(w.reshape(N, 128, 2048), rng)
    return {"wc": c, "ws": p}
def setup_inputs(rng):
    return {**numbers_of(rng), **weights(rng)}
def setup_inputs_ties(rng):
    d = numbers_of(rng)
    e = rng.permutation(N)
    x = d["x"].reshape(N, 8, 16, C, 4)
    a = x[0][:, :8, :3].copy()
    a[:, :, 2] = 0
    for r in range(N):
        k = np.zeros(C, int) if r == e[0] else rng.permutation(C) % 3
        x[r][:, :8] = a[:, :, k]
    x[e[1]] = 0
    u = d["u"].reshape(N, 8, 16, 128, 4)
    u[1:, :, :, ::32] = u[:1, :, :, ::32].copy()
    u[:, :, 8:, ::16] = 0
    return {"x": x.reshape(N, 128, 4 * C), "u": u.reshape(N, 128, 512), "v": d["v"], **weights(rng, range(8))}
def setup_inputs_near(rng):
    d = numbers_of(rng)
    x = d["x"].astype(np.float32).reshape(N, 8, 16, C, 4)
    u = d["u"].reshape(N, 128, 128, 4)
    u[:, :, ::16] = 0
    x[:, :, 0] = 0
    o = rng.permutation(8) % 4
    for r in range(N):
        for g in range(8):
            size = 2.0 ** -7 if o[g] == 3 else 1.0
            sign = -1.0 if r % 2 == 1 and o[g] < 3 else 1.0
            s = rng.integers(0, 256, C)
            b = ((s[:, None] >> np.arange(8)) & 1) * np.exp2(np.arange(8) - 23.0) * size * sign
            x[r, g, 8] = b[:, :4]
            x[r, g, 9] = b[:, 4:]
            x[r, g, 10:] = rng.integers(4, 8, (6, C, 4)) * 2.0 ** -20 * size
            if sign < 0: x[r, g, 0, :, 0] = -1
            if o[g] % 2 == 0 or o[g] == 3 and r % 2 == 0: x[r, g, 0, int(rng.integers(C)), 0] = sign * 2.0 ** 30
            k = 2.0 ** -30 if o[g] >= 2 else 1.0
            u[r, 16 * g, 16 * g, 0] = 1.0 if o[g] == 3 else k
            u[r, 16 * g + 8:16 * g + 10, 16 * g] = k
            if sign < 0 and r % 4 == 1:
                x[r, g, 0, :, 1] = -2.0 ** -9
                u[r, 16 * g, 16 * g, 1] = k
            if o[g] == 3:
                h = rng.integers(0, 6, C)
                x[r, g, 10, :, 0] = (8 + h) * 2.0 ** -33
                x[r, g, 11, :, 0] = (9 + h) * 2.0 ** -33
                u[r, 16 * g + 10, 16 * g, 0] = 9 * 2.0 ** -33
                u[r, 16 * g + 11, 16 * g, 0] = -8 * 2.0 ** -33
    return {"x": x.reshape(N, 128, 4 * C).astype(BF), "u": u.reshape(N, 128, 512), "v": d["v"], **weights(rng, [0, 8, 9, 10, 11, 12, 13, 14, 15])}
def setup_inputs_lags(rng):
    d = numbers_of(rng)
    x = d["x"].astype(np.float32).reshape(N, 8, 16, C, 4)
    u = d["u"].reshape(N, 128, 128, 4)
    size = np.where(rng.permutation(N) < N // 2, 2.0 ** -30, 1.0).astype(np.float32)
    x[:, :, :11] = 0
    ring = np.argsort(rng.random((8, C)), axis=1)
    key = np.zeros((N, 8, C), int)
    full, first = rng.permutation(8) < 4, rng.integers(0, S, 8)
    kept = [0, 1, 3, 4] if S == 8 else [0, 1, 3]
    for r in range(N):
        n = rng.permutation([0, 1, 2, 3, C // 2 + 2, 257, C - 1, C])
        for g in range(8):
            a = np.where(rng.permutation(C) < n[g], 1, -rng.integers(0, 2, C)) * size[r]
            x[r, g, 0, :, 0] = a * 1.125
            x[r, g, 1, :, 0] = a * 1.25
            gone, new = rng.permutation(C) < C // 4, rng.permutation(C)
            if full[g]: gone, new = ~np.isin((np.arange(C) - first[g]) % S, kept), new + 512 * (r % 2)
            key[r, g] = np.where(gone, new, np.roll(ring[g], S * int(rng.integers(M))))
    z = ((key[:, :, :, None] >> np.arange(12)) & 1) * np.exp2(np.arange(12.0))
    for i in range(3): x[:, :, 8 + i] = z[:, :, :, 4 * i:4 * i + 4]
    u[:, :, ::16] = 0
    u[:, :, 1::16] = 0
    for h in range(0, 128, 16):
        u[:, h + 8:h + 11, h] = 1
        u[:, h, h + 1, 0] = (size * np.float32(1.125)).astype(BF)
        u[:, h + 1, h + 1, 0] = (-size).astype(BF)
    return {"x": x.reshape(N, 128, 4 * C).astype(BF), "u": u.reshape(N, 128, 512), "v": d["v"], **weights(rng, range(11))}
def setup_inputs_huge(rng):
    d = numbers_of(rng)
    x = 2.0 ** 30 * (0.9 + 0.1 * rng.random((N, 128, C, 4)))
    x[:, ::8] = 2.0 ** 30
    far, c = rng.permutation(8) % 2, rng.permutation(8) % 2 * 2.0 - 1.0
    u = d["u"].reshape(N, 128, 8, 16, 4)
    for r in range(N):
        k = np.where((far == 1) & (r % 2 == 1), -c, c)
        a = 2.0 ** 30 * (1 - 0.05 * rng.random((128, 8, 4)))
        a[::8] = 2.0 ** 30
        u[r, :, :, 0] = (a * k[:, None]).astype(np.float32).astype(BF)
    w = np.zeros((N, 128, 4, 128, 4), np.float32)
    i = np.flatnonzero(np.arange(128) % 8)
    for b in range(4): w[:, i, b, i, b] = -1
    wc, ws = packed(w.reshape(N, 128, 2048).astype(BF), rng)
    return {"x": x.astype(np.float32).reshape(N, 128, 4 * C).astype(BF), "u": u.reshape(N, 128, 512), "v": d["v"], "wc": wc, "ws": ws}
def setup_inputs_spread(rng):
    d = setup_inputs(rng)
    d["x"] = big(wide(rng, N, 128, 4 * C, cols=6))
    return d
def check_inputs(d):
    b = []
    for k in ("x", "u", "v"):
        a = np.abs(d[k].astype(np.float32))
        if not (np.isfinite(a).all() and ((a == 0) | (a >= 2.0 ** -30) & (a <= 2.0 ** 30)).all()): b.append("a value of " + k)
    none, least, most = [emit(mx_ref.quantize(np.full((128, 16), k, np.float32).astype(BF)))[1][0, 0] for k in (0.0, 2.0 ** -30, 2.0 ** 30)]
    for r in range(N):
        if ((d["wc"][r] == 0x7F) | (d["wc"][r] == 0xFF)).any(): b.append("wc: a code that is no number")
        s = mx_ref.live(d["ws"][r])
        if ((s != none) & ((s < least) | (s > most))).any(): b.append("ws: a scale out of range")
        if ((s == none) & ((d["wc"][r].reshape(16, 8, -1, 4) & 0x7F) != 0).any(axis=(1, 3))).any(): b.append("wc: a code that isn't zero under the scale of zeros")
    return b
def reference(x, u, v, wc, ws):
    qu = [mx_ref.quantize(u[r]) for r in range(N)]
    lay = [pk(wc[r], ws[r]) for r in range(N)]
    now = [x[r] for r in range(N)]
    for t in range(R):
        sent = [mx_ref.quantize(now[r]) for r in range(N)]
        p = [mx_ref.matmul(qu[r], sent[r]) for r in range(N)]
        came = decode(join(*sent)).astype(BF)
        made, places = [], []
        for r in range(N):
            s = (r + STEP[t]) % N
            lag = 1 + np.sum(p[r][1::16] > 0, axis=1) % 4
            e, m = match(p[r][::16], p[s][::16], lag)
            q = mx_ref.quantize(gcols(cut(came, s, 4 * C), (m + H) % C))
            own = gcols(now[r], e)
            h = tile([mx_ref.matmul(pick(lay[r], np.arange(128 * b, 128 * b + 128)), q) * np.float32(0.015625) + own[:, b::4].astype(np.float32) for b in range(4)])
            made.append(gput(now[r], e, h))
            places.append(e)
        now = made
    y, oe = np.zeros((N, 128, C), np.float32), np.zeros((N, 8, K), np.float32)
    oc, osc = np.zeros((N, 128, 4 * C), np.uint8), np.zeros((N, 16, C), np.uint8)
    for r in range(N):
        q = mx_ref.quantize(now[r])
        y[r] = mx_ref.matmul(mx_ref.quantize(v[r]), q)
        oe[r] = places[r]
        oc[r], osc[r] = emit(q)
    return {"y": y, "oe": oe, "oc": oc, "osc": osc}

from concourse.bass import DstId, RemoteDMATransfer
from concourse.mybir import dt, AluOpType, AxisListType, ActivationFunctionType

C, K, M, S, H, R = 320, 128, 64, 5, 7, 3
STEP = [1, 3, 1]
DW = 336
JW = 3392
F32, BF, I32, U16, Q8, U8 = "float32", "bfloat16", "int32", "uint16", "float8_e4m3fn_x4", "uint8"


def sb(n, d):
    return ("sbuf", [128, n], d)


SCRATCH = {
    "X": sb(4 * C, BF), "ut": sb(512, BF), "vt": sb(512, BF),
    "wq": sb(512, Q8), "wsc": sb(512, U8),
    "qu": sb(128, Q8), "su": sb(128, U8), "qv": sb(128, Q8), "sv": sb(128, U8),
    "qu16": sb(16, Q8), "su16": sb(16, U8), "qur": sb(256, Q8), "sur": sb(256, U8),
    "lqa": sb(16, Q8), "lsa": sb(16, U8), "lqb": sb(16, Q8), "lsb": sb(16, U8),
    "qra": sb(128, Q8), "sra": sb(128, U8), "qrb": sb(128, Q8), "srb": sb(128, U8),
    "et": sb(2048, BF), "qe": sb(512, Q8), "se": sb(512, U8),
    "zt": sb(512, BF), "qz": sb(128, Q8), "sz": sb(128, U8),
    "p0": ("psum", [128, 512], F32), "p1": ("psum", [128, 512], F32), "pl": ("psum", [128, 512], F32),
    "pd": ("psum", [128, 2048], F32),
    "ip": sb(8, I32), "idn": sb(128, F32), "one": sb(128, F32), "bci": sb(16, I32), "ti": sb(32, I32), "rs20": sb(400, BF),
    "ps": sb(C, F32), "sg": sb(C, BF), "sg2": sb(C, BF), "cnt": sb(8, F32), "cti": sb(8, I32), "pm": sb(384, F32), "pn": sb(384, F32),
    "l1": sb(40, F32), "l2": sb(40, F32), "l3": sb(40, F32), "o_mx": sb(40, U16),
    "A": sb(28 * M, F32), "dd": sb(20 * M, F32), "sm": sb(20 * M, F32), "jk": sb(20 * M, BF), "am": sb(20, F32),
    "bc": sb(640, F32), "tb": sb(640, F32), "ab": sb(C, F32),
    "dl": sb(40, F32), "rp": sb(400, F32), "lf": sb(400, BF), "lr": sb(400, BF),
    "e1": sb(128, F32), "e2": sb(128, F32), "pv": sb(128, F32), "li": sb(48, F32), "li3": sb(48, F32),
    "e3": sb(48, F32), "e4": sb(48, F32), "pw": sb(48, F32), "f1": sb(8, F32), "qq": sb(8, F32), "dr": sb(48, F32),
    "fl": sb(8 * C, BF), "fs": sb(8 * C, BF), "rk": sb(8, F32),
    "m1": sb(20, F32), "m2": sb(20, F32), "mx": sb(C, F32),
    "sel": sb(20, F32), "loc": sb(20, F32), "lt": sb(32, F32), "ltt": sb(32, F32), "bs": sb(8, F32),
    "g1": sb(20, F32), "g3": sb(20, F32), "o_d": sb(20, U16),
    "win": sb(JW, F32), "tw": sb(256, F32), "ts": sb(256, F32),
    "o_z": sb(32, U16), "vb": sb(32, F32), "zf": sb(32, F32), "de": sb(32, F32), "o_e": sb(32, U16),
    "ds": sb(4 * DW, BF), "rsb": sb(512, F32), "gt": sb(512, BF),
    "ef": sb(32, F32), "eft": sb(32, F32), "ys": sb(C, F32),
}
for _t in range(R + 1):
    SCRATCH["qx%d" % _t] = sb(C, Q8)
    SCRATCH["sx%d" % _t] = sb(C, U8)
for _t in range(R):
    SCRATCH["lq%d" % _t] = sb(C, Q8)
    SCRATCH["ls%d" % _t] = sb(C, U8)

PART = {}
for _buf, _d, _parts in (
        ("kf", F32, [("pc", 16), ("i32", 32), ("cf", 224), ("tmpc", 512), ("t16", 64), ("msk", 384), ("rs16", 384), ("fb", C),
                     ("rs64", 256), ("base", 40), ("cc", 40), ("mzc", 20), ("lm", 32), ("jf", 20), ("bq", 32), ("rho", 200),
                     ("thr", 8), ("ones", 20)]),
        ("ko", U16, [("o_u", 2), ("o_rep", 16), ("o_t", 20), ("o_pn", 24), ("o_j", 24), ("o_bc", 8), ("o_sel", 20),
                     ("o_fin", 2), ("o_a", 26), ("o_b", 26), ("o_c", 8), ("o_l", 8)])):
    _at = 0
    for _n, _w in _parts:
        PART[_n] = (_buf, _at, _w)
        _at += (_w + 15) // 16 * 16
    SCRATCH[_buf] = sb(_at, _d)

NDMA = 24
SEMAPHORES = ["cv", "cs", "ct", "cg", "left", "au", "a0", "a1", "a2"] + ["d%d" % _k for _k in range(NDMA)]


def rank_program(g, core, T, topo):
    rank = T.rank_of(core)
    if rank is None:
        return
    N = len(T.cores)
    A_, ACT = AluOpType, ActivationFunctionType
    Q = {"v": g.vector, "s": g.scalar, "t": g.tensor, "g": g, "y": g.sync}
    CSEM = {"v": "cv", "s": "cs", "t": "ct", "g": "cg"}
    total = {}
    seen = {q: {} for q in Q}
    hist = {}
    ndma = [0]

    def V(name, lo=0, hi=None, step=1):
        if name in PART:
            buf, at0, w = PART[name]
            return (buf, at0 + lo, at0 + (w if hi is None else hi), step)
        return (name, lo, SCRATCH[name][1][1] if hi is None else hi, step)

    def col(name, j):
        return V(name, j, j + 1)

    def ap(v):
        if not isinstance(v, tuple):
            return v
        if v[0] == "*":
            w = ap(v[1])
            if SCRATCH[v[1][0]][2] == Q8:
                w = w.bitcast(dt.uint32)
            return w.indirect(ap(v[2]))
        return T[v[0]][:, v[1]:v[2]:v[3]] if v[3] != 1 else T[v[0]][:, v[1]:v[2]]

    def meet(a, b):
        if SCRATCH[a[0]][0] == "psum":
            return a[1] // 512 == b[1] // 512
        if a[2] <= b[1] or b[2] <= a[1]:
            return False
        if a[3] == b[3] and a[3] > 1:
            return (a[1] - b[1]) % a[3] == 0
        return True

    def wait(q, tok):
        sem, val, clock = tok
        if seen[q].get(sem, 0) >= val:
            return
        Q[q].wait_ge(T.sem[sem], val)
        seen[q][sem] = val
        for k, x in clock.items():
            if seen[q].get(k, 0) < x:
                seen[q][k] = x

    def flat(vs):
        out = []
        for v in vs:
            if isinstance(v, tuple):
                out += [v[1], v[2]] if v[0] == "*" else [v]
        return out

    def order(q, reads, writes):
        need = []
        for v, w in [(v, False) for v in reads] + [(v, True) for v in writes]:
            ps = SCRATCH[v[0]][0] == "psum"
            for r, tok, wrote, oq in hist.get(v[0], []):
                if (wrote or w or (ps and oq != q)) and meet(v, r):
                    need.append(tok)
        for tok in sorted(need, key=lambda k: -k[1]):
            wait(q, tok)

    def note(q, reads, writes, tok):
        for v in writes:
            hist[v[0]] = [e for e in hist.get(v[0], []) if not (e[0][1] >= v[1] and e[0][2] <= v[2] and (v[3] == 1 or e[0] == v))]
            hist[v[0]].append((v, tok, True, q))
        for v in reads:
            hist.setdefault(v[0], []).append((v, tok, False, q))

    def op(q, call, outs, ins):
        wr, rd = [], flat(ins)
        for o in outs:
            if o[0] == "*":
                wr.append(o[1])
                rd.append(o[2])
            else:
                wr.append(o)
        order(q, rd, wr)
        sem = CSEM[q]
        call().then_inc(T.sem[sem], 1)
        total[sem] = total.get(sem, 0) + 1
        note(q, rd, wr, (sem, total[sem], dict(seen[q])))

    def dma(q, out, in_, outs, ins):
        order(q, ins, outs)
        sem = "d%d" % ndma[0]
        ndma[0] += 1
        Q[q].dma_start(out, in_).then_inc(T.sem[sem], 16)
        total[sem] = 16
        note(q, ins, outs, (sem, 16, dict(seen[q])))

    def arrives(sem, n, views):
        total[sem] = n
        note("far", [], views, (sem, n, {}))

    def ts(o, a, s1, op0, s2=None, op1=None):
        if op1 is None:
            op("v", lambda: g.vector.tensor_scalar(ap(o), ap(a), ap(s1), None, op0), [o], [a, s1])
        else:
            op("v", lambda: g.vector.tensor_scalar(ap(o), ap(a), ap(s1), ap(s2), op0, op1), [o], [a, s1, s2])

    def tt(o, a, b, f):
        op("v", lambda: g.vector.tensor_tensor(ap(o), ap(a), ap(b), f), [o], [a, b])

    def cp(o, a):
        if o[0] != "*" and SCRATCH[o[0]][2] == Q8:
            op("v", lambda: g.vector.tensor_copy(ap(o).bitcast(dt.uint32), ap(a)), [o], [a])
        else:
            op("v", lambda: g.vector.tensor_copy(ap(o), ap(a)), [o], [a])

    def scan(o, a, b, init, op0, op1):
        op("v", lambda: g.vector.tensor_tensor_scan(ap(o), ap(a), ap(b), init, op0, op1), [o], [a, b])

    def tr(o, a):
        op("v", lambda: g.vector.transpose(ap(o), ap(a)), [o], [a])

    def reduce(o, a):
        op("v", lambda: g.vector.tensor_reduce(ap(o), ap(a), AxisListType.X, A_.add), [o], [a])

    def ms(o, c):
        op("v", lambda: g.vector.memset(ap(o), c), [o], [])

    def quant(qn, sn, a):
        op("v", lambda: g.vector.quantize_mx(ap(qn), ap(sn), ap(a)), [qn, sn], [a])

    def act(o, a, f, bias=None, scale=None, acc=None):
        kw = {}
        if bias is not None:
            kw["bias"] = ap(bias)
        if scale is not None:
            kw["scale"] = scale
        if acc is not None:
            kw["accum_out"] = ap(acc)
        op("s", lambda: g.scalar.activation(ap(o), ap(a), f, **kw), [o] + ([acc] if acc else []), [a, bias])

    def mm(o, wq, ws, xq, xs):
        op("t", lambda: g.tensor.matmul_mx(ap(o), ap(wq), ap(ws), ap(xq), ap(xs), True, True), [o], [wq, ws, xq, xs])

    def iota(o, pat, base=0, ch=0):
        if SCRATCH[o[0]][2] == I32:
            op("g", lambda: g.iota(ap(o), pat, base, ch), [o], [])
        else:
            op("g", lambda: g.iota(ap(o), pat, base, ch, allow_small_or_imprecise_dtypes=True), [o], [])

    def raw(v):
        return ap(v).bitcast(dt.uint8) if SCRATCH[v[0]][2] == Q8 else ap(v)

    def engines(sender, dests):
        m = topo.mask(sender, dests[0])
        for c in dests[1:]:
            m &= topo.mask(sender, c)
        return m

    def share(sender, dests):
        return bin(engines(sender, dests)).count("1")

    def send(src, dsts, sem):
        order("g", [src], [])
        m = engines(core, [c for c, _ in dsts])
        if len(dsts) == 1:
            rid, pid, _ = topo.addr(dsts[0][0])
            g.remote_dma(raw(dsts[0][1]), raw(src), T.sem[sem], T.sem.left, pid, rid, m)
        else:
            ids = [DstId(rid=topo.addr(c)[0], pnc=topo.addr(c)[1]) for c, _ in dsts]
            g.remote_dma_fused([RemoteDMATransfer(dst_ids=ids, dma_engine_mask=m, remote_sem=T.sem[sem], src=raw(src),
                                                  dsts=[raw(v) for _, v in dsts])], local_sem=T.sem.left)
        total["left"] = total.get("left", 0) + bin(m).count("1")

    def at(r):
        return T.cores[r % N]

    dma("y", T.ut[:], T.u[:], [V("ut")], [])
    dma("s", T.X[:], T.x[:], [V("X")], [])

    iota(col("ip", 0), [[0, 1]], 0, 1)
    iota(V("i32"), [[1, 32]])
    iota(V("idn"), [[-1, 128]], 0, 1)
    iota(V("cf", 96, 136), [[1, 5], [0, 8]])
    iota(V("cf", 136, 176), [[0, 10], [1, 4]])
    iota(V("cf", 176, 216), [[0, 5], [16, 8]])
    iota(V("cf", 40, 60), [[0, 4], [1, 5]], H)
    iota(V("cf", 64, 96), [[1, 4], [0, 8]])
    iota(V("bci", 0, 8), [[M, 4], [0, 2]], M - 1)
    J, P31, H16 = col("pc", 0), col("pc", 1), col("pc", 6)
    p = col("ip", 0)
    ms(V("rs64"), 0.0)
    ts(col("ip", 1), p, 15, A_.bitwise_and)
    ts(col("ip", 2), p, 31, A_.bitwise_and)
    ts(col("ip", 3), p, 7, A_.bitwise_and)
    ts(col("ip", 4), p, 3, A_.logical_shift_right, 1, A_.bitwise_and)
    ts(col("ip", 5), p, 1, A_.bitwise_and)
    ts(col("ip", 6), p, 1, A_.logical_shift_right, 3, A_.bitwise_and)
    ts(col("ip", 7), p, 16, A_.bitwise_and)
    ts(V("o_rep", 0, 8), V("i32", 0, 8), 16.0, A_.mult)
    cp(V("pc", 0, 7), V("ip", 1, 8))
    ts(V("o_rep", 8, 16), V("i32", 0, 8), 16.0, A_.mult, 1.0, A_.add)
    ts(V("t16", 16, 32), V("i32", 0, 16), 0.0, A_.is_gt)
    ts(V("o_j"), V("i32", 0, 24), 0.0, A_.mult, J, A_.add)
    ts(V("t16", 0, 16), V("i32", 0, 16), J, A_.is_equal)
    ts(col("o_u", 0), col("pc", 2), 16.0, A_.mult, col("pc", 3), A_.add)
    act(V("msk"), ("*", V("t16", 0, 16), V("o_j")), ACT.Copy)
    act(V("rs16"), ("*", V("t16", 16, 32), V("o_j")), ACT.Copy)
    ts(V("one"), V("idn"), 0.0, A_.is_equal)
    cp(V("o_t"), V("i32", 0, 20))
    ts(col("pc", 7), J, 20.0, A_.mult)
    ts(col("pc", 8), J, 8.0 * M, A_.add)
    ts(V("tmpc", 112, 138), V("i32", 0, 26), 16.0, A_.mult, J, A_.add)
    ts(V("tmpc", 0, 24), V("i32", 0, 24), col("pc", 7), A_.add, -4.0, A_.add)
    ts(V("t16", 48, 64), V("i32", 0, 16), J, A_.is_lt, -2.0 ** -24, A_.mult)
    ts(V("ti", 0, 26), V("tmpc", 112, 138), -9.5, A_.add, 0.05, A_.mult)
    ts(V("tmpc", 24, 48), V("tmpc", 0, 24), 0.0, A_.is_lt, float(C), A_.mult)
    ts(V("t16", 48, 64), V("t16", 48, 64), 1.0, A_.add)
    ts(V("tmpc", 72, 112), V("cf", 136, 176), J, A_.add, 0.0, A_.is_equal)
    tt(V("tmpc", 48, 72), V("tmpc", 0, 24), V("tmpc", 24, 48), A_.add)
    ts(V("base"), V("cf", 176, 216), col("pc", 8), A_.add)
    tt(V("t16", 32, 48), V("t16", 48, 64), V("t16", 0, 16), A_.subtract)
    cp(V("o_pn"), V("tmpc", 48, 72))
    ts(V("cc"), V("tmpc", 72, 112), -float(M), A_.mult, 1.0, A_.add)
    ts(V("tmpc", 140, 166), V("ti", 0, 26), -20.0, A_.mult)
    cp(V("tmpc", 168, 194), V("ti", 0, 26))
    cp(V("o_b"), V("ti", 0, 26))
    ms(V("rs64", 0, 256, M), 1e29)
    tt(V("tmpc", 196, 222), V("tmpc", 112, 138), V("tmpc", 140, 166), A_.add)
    cp(V("o_bc"), V("bci", 0, 8))
    ts(V("o_sel"), V("i32", 0, 20), 32.0, A_.mult, P31, A_.add)

    def tiles_e(bs):
        for b in bs:
            for k in range(4):
                act(V("et", 512 * b + k, 512 * b + 512, 4), V("one"), ACT.Copy, scale=1.0 if k == b else 0.0)

    quant(V("qu"), V("su"), V("ut"))
    tt(V("tmpc", 224, 250), V("tmpc", 196, 222), V("tmpc", 168, 194), A_.is_lt)
    cp(V("qu16"), ("*", V("qu"), V("o_u", 0, 1)))
    cp(V("su16"), ("*", V("su"), V("o_u", 0, 1)))
    askers = [(at(rank - 1), "a"), (at(rank - 3), "b")]
    send(V("qu16"), [(c, V("lq" + k)) for c, k in askers], "au")
    send(V("su16"), [(c, V("ls" + k)) for c, k in askers], "au")
    arrives("au", sum(2 * share(at(r), [at(r - 1), at(r - 3)]) for r in (rank + 1, rank + 3)),
            [V("lqa"), V("lsa"), V("lqb"), V("lsb")])
    act(V("sur"), ("*", V("su"), V("o_rep")), ACT.Copy)
    tiles_e([0, 1])
    cp(V("qur"), ("*", V("qu"), V("o_rep")))
    ts(V("tmpc", 252, 278), V("tmpc", 224, 250), 20.0, A_.mult)
    cp(V("o_c"), V("tmpc", 196, 204))

    def publish(t):
        quant(V("qx%d" % t), V("sx%d" % t), V("X"))
        to = at(rank - STEP[t])
        send(V("qx%d" % t), [(to, V("lq%d" % t))], "a%d" % t)
        send(V("sx%d" % t), [(to, V("ls%d" % t))], "a%d" % t)
        arrives("a%d" % t, 2 * share(at(rank + STEP[t]), [core]), [V("lq%d" % t), V("ls%d" % t)])

    publish(0)
    iota(V("rho", 0, 140), [[3, 7], [0, 20]], 2)
    iota(V("rho", 140, 200), [[1, 3], [0, 20]])
    dma("y", T.wq[:].bitcast(dt.uint8), T.wc[:], [V("wq")], [V("lq0")])
    dma("y", T.wsc[:], T.ws[:], [V("wsc")], [])
    dma("y", T.vt[:], T.v[:], [V("vt")], [])
    ts(V("o_l"), V("tmpc", 196, 204), 20.0, A_.mult, 19.0, A_.add)
    tt(V("tmpc", 280, 306), V("tmpc", 252, 278), V("tmpc", 196, 222), A_.add)
    ts(col("pc", 9), J, 200.0, A_.mult, 160.0, A_.add)
    ts(col("pc", 10), H16, 16.0, A_.add)
    ts(col("pc", 11), H16, -1.0, A_.add)
    ts(col("pc", 12), col("pc", 4), 128.0, A_.mult, H16, A_.add)
    cp(V("o_a"), V("tmpc", 280, 306))
    ts(V("tmpc", 420, 440), V("i32", 0, 20), col("pc", 7), A_.add, 1.0 / 1024, A_.mult)
    ts(V("tmpc", 440, 472), V("i32"), P31, A_.is_gt)

    def late_constants():
        act(V("sra"), ("*", V("lsa"), V("o_t", 0, 8)), ACT.Copy)
        tiles_e([2, 3])
        cp(V("qra"), ("*", V("lqa"), V("o_t", 0, 8)))

    def later_constants():
        ts(V("tmpc", 472, 504), V("i32"), col("pc", 10), A_.is_lt)
        ts(col("pc", 13), col("pc", 5), 32.0, A_.mult, col("pc", 12), A_.add)
        tt(V("mzc"), V("tmpc", 420, 440), V("cf", 40, 60), A_.add)
        ts(V("jf"), V("i32", 0, 20), col("pc", 9), A_.add)
        ts(V("bq"), V("cf", 64, 96), 1.0 / 4096, A_.mult)
        tt(V("lm"), V("tmpc", 440, 472), V("tmpc", 472, 504), A_.mult)
        ts(col("pc", 14), col("pc", 13), 15.0, A_.add)
        ms(V("rs20"), 1.0)
        ts(V("thr"), V("i32", 0, 8), -3.0, A_.mult, K + 18.0, A_.add)
        ms(V("ones"), 1.0)
        ts(V("o_fin"), V("i32", 0, 2), 0.0, A_.mult, col("pc", 14), A_.add)
        ms(V("rs20", 0, 400, 20), 0.0)
        ms(V("win", 0, 160), 0.0)
        quant(V("qe"), V("se"), V("et"))

    for t in range(R):
        qx, sx, lq, ls = V("qx%d" % t), V("sx%d" % t), V("lq%d" % t), V("ls%d" % t)
        lib = "a" if STEP[t] == 1 else "b"
        mm(V("p0", 0, C), V("qur", 0, 128), V("sur", 0, 128), qx, sx)
        mm(V("p1", 0, C), V("qur", 128, 256), V("sur", 128, 256), qx, sx)
        act(V("ps"), V("p0", 0, C), ACT.Copy)
        act(V("sg"), V("p1", 0, C), ACT.Sign)
        act(V("sg2"), V("sg"), ACT.Relu, acc=col("cnt", 0))
        tt(V("pm"), ("*", V("ps"), V("o_pn")), V("msk"), A_.mult)
        scan(V("pn"), V("rs16"), V("pm"), 0.0, A_.mult, A_.add)
        cp(col("cti", 0), col("cnt", 0))
        if t == 0:
            late_constants()
        ts(col("cti", 1), col("cti", 0), 3, A_.bitwise_and)
        ts(col("cnt", 1), col("cti", 1), 1.0, A_.add)
        ts(col("cnt", 2), col("cti", 1), -2.0 * M, A_.mult, -2.0 * M, A_.add)
        ts(V("l1"), V("cf", 96, 136), col("cnt", 1), A_.is_lt)
        tt(V("l2"), V("l1"), V("cc"), A_.mult)
        tt(V("l3"), V("base"), V("l2"), A_.subtract)
        ts(V("o_mx"), V("l3"), col("cnt", 2), A_.add)
        if t == 0:
            later_constants()
        mm(V("pl", 0, C), V("qr" + lib), V("sr" + lib), lq, ls)
        for b in range(4):
            mm(V("pd", 512 * b, 512 * b + C), V("qe", 128 * b, 128 * b + 128), V("se", 128 * b, 128 * b + 128), lq, ls)

        W = 2 * M

        def dist(lo, hi):
            for u in range(lo, hi):
                for hf in range(2):
                    k = u + 4 + 10 * hf
                    act(V("A", W * (u + 4) + M * hf, W * (u + 4) + M * hf + M), V("pl", u % S, C, S), ACT.Abs,
                        bias=col("pn", 16 * k + 15), scale=-1.0)

        def larger(u):
            tt(V("dd", W * u, W * u + W), ("*", V("A", W * u, W * u + 4 * W), V("o_mx", 8 * (u % S), 8 * (u % S) + 8)),
               V("A", W * (u + 4), W * (u + 5)), A_.max)

        def least(c):
            scan(V("sm", 256 * c, 256 * c + 256), V("rs64"), V("dd", 256 * c, 256 * c + 256), 0.0, A_.add, A_.min)

        def spread(c):
            act(V("bc", 128 * c, 128 * c + 128), ("*", V("sm", 256 * c, 256 * c + 256), V("o_bc")), ACT.Identity, bias=2.0 ** -120)

        def first(c):
            for k in range(4 * c, 4 * c + 4):
                act(V("jk", M * k, M * k + M), V("sm", M * k, M * k + M), ACT.Sign, bias=col("sm", M * k + M - 1), scale=-1.0,
                    acc=col("am", k // 2 + 10 * (k % 2)))

        def turn(c):
            tr(V("tb", 128 * c, 128 * c + 128), V("bc", 128 * c, 128 * c + 128))

        dist(-4, 6); larger(0); larger(1); larger(2); least(0); larger(3); spread(0); dist(6, 8)
        larger(4); least(1); larger(5); turn(0); spread(1); dist(8, 10); larger(6); least(2); larger(7); turn(1)
        if t == 0:
            act(V("fb"), ("*", V("t16", 32, 48), V("o_j", 0, 20)), ACT.Copy)
        first(0); spread(2); larger(8); least(3); larger(9); turn(2); first(1); spread(3); least(4); spread(4)

        for hf in range(2):
            ts(V("dl", 10 * hf, 10 * hf + 10), V("sm", M * hf + M - 1, 20 * M, W), 2.0 ** -120, A_.add)
        turn(3)
        for hf in range(2):
            ts(V("dl", 20 + 10 * hf, 30 + 10 * hf), V("sm", M * hf + M - 1, 20 * M, W), 2.0 ** -120, A_.add, 1.0 - 2.0 ** -24, A_.mult)
        act(V("rp"), ("*", V("dl", 0, 20), V("o_b", 0, 25)), ACT.Copy)
        turn(4)
        tt(V("ab"), ("*", V("tb"), V("o_sel")), V("fb"), A_.mult)
        tt(V("lf"), ("*", V("dl"), V("o_a", 0, 25)), V("rp"), A_.is_lt)
        first(2); first(3); first(4)
        scan(V("lr"), V("rs20"), V("lf"), 0.0, A_.mult, A_.add)
        LR = V("lr", 19, 400, 20)
        act(V("m1"), V("am"), ACT.Copy, scale=-float(S))
        act(V("dr"), ("*", V("dl", 0, 20), V("o_c", 0, 3)), ACT.Copy)

        def cmpv(k, c):
            ts(V("fl", C * k, C * k + C), V("ab"), c, A_.is_lt)

        def sumv(k):
            scan(V("fs", C * k, C * k + C), V("fl", C * k, C * k + C), V("fl", C * k, C * k + C), 0.0, A_.add, A_.max)

        def cmps(k, c):
            act(V("fl", C * k, C * k + C), V("ab"), ACT.Sign, bias=c, scale=-1.0)

        def sums(k):
            act(V("fs", C * k, C * k + C), V("fl", C * k, C * k + C), ACT.Relu, acc=col("rk", k))

        tt(V("e1"), ("*", V("lr"), V("o_l")), V("rho", 0, 128), A_.is_equal)
        tt(V("li"), ("*", V("lr"), V("o_l", 0, 3)), V("rho", 140, 188), A_.subtract)
        tt(V("e2"), ("*", V("dl", 0, 20), V("o_c")), V("e1"), A_.mult)
        ts(V("li3"), V("li"), 1.0 / 3, A_.mult)
        scan(V("pv"), V("rs20", 0, 128), V("e2"), 0.0, A_.mult, A_.add)
        tt(V("m2"), V("m1"), V("mzc"), A_.add)
        pv = [col("pv", 20 * k + 19) for k in range(6)]
        cmps(3, pv[3]); cmps(4, pv[4]); sums(3); cmps(5, pv[5]); sums(4); sums(5)
        cmpv(0, pv[0]); cmpv(1, pv[1]); sumv(0); cmpv(2, pv[2]); sumv(1); sumv(2)
        tt(V("mx"), ("*", V("m2"), V("o_t")), V("msk", 0, C), A_.mult)
        tt(V("f1", 0, 3), V("fs", C - 1, 3 * C, C), V("thr", 0, 3), A_.is_lt)
        tt(V("f1", 3, 6), V("rk", 3, 6), V("thr", 3, 6), A_.is_lt)
        reduce(col("qq", 0), V("f1", 0, 6))
        ts(V("e3"), V("li3"), col("qq", 0), A_.is_equal)
        ts(col("qq", 1), col("qq", 0), 3.0, A_.mult)
        tt(V("e4"), V("e3"), V("dr"), A_.mult)
        ts(col("qq", 2), col("qq", 0), -3.0, A_.mult, K + 20.0, A_.add)
        scan(V("pw"), V("rs20", 0, 48), V("e4"), 0.0, A_.mult, A_.add)
        ts(col("qq", 3), col("qq", 0), -3.0, A_.mult, K + 19.0, A_.add)
        act(V("ds", 0, C), V("pd", 0, C), ACT.Copy)
        cmps(7, col("pw", 39)); sums(7)
        cmpv(6, col("pw", 19))
        for b in range(4):
            if b:
                act(V("ds", DW * b, DW * b + C), V("pd", 512 * b, 512 * b + C), ACT.Copy)
            act(V("ds", DW * b + C, DW * b + C + H), V("pd", 512 * b, 512 * b + H), ACT.Copy)
        sumv(6)
        ts(col("qq", 4), col("fs", 7 * C - 1), col("qq", 2), A_.is_lt, col("qq", 1), A_.add)
        ts(col("qq", 5), col("rk", 7), col("qq", 3), A_.is_lt, col("qq", 4), A_.add)

        ts(V("lt"), V("lm"), col("qq", 5), A_.mult)
        ts(V("sel"), LR, col("qq", 5), A_.is_ge)
        tr(V("ltt"), V("lt"))
        scan(V("loc"), V("ones"), V("sel"), 0.0, A_.add, A_.subtract)
        tt(V("g1"), V("sel"), V("jf"), A_.mult)
        reduce(col("bs", 0), V("ltt"))
        tt(V("g3"), V("g1"), V("loc"), A_.add)
        ts(V("o_d"), V("g3"), col("bs", 0), A_.add, col("pc", 11), A_.add)
        cp(("*", V("win"), V("o_d")), V("mx"))
        tr(V("tw", 0, 128), V("win", 0, 128))
        tr(V("tw", 128, 256), V("win", 16, 144))
        scan(V("ts"), V("rs16", 0, 256), V("tw"), 0.0, A_.mult, A_.add)
        cp(V("o_z"), ("*", V("ts"), V("o_fin")))
        tt(V("vb"), ("*", V("ts"), V("o_fin")), V("bq"), A_.add)

        for b in (2, 3):
            act(V("zt", b, 512, 4), ("*", V("ds", DW * b, DW * b + C + H), V("o_z", 0, 8)), ACT.Copy)
        for b in (0, 1):
            cp(V("zt", b, 512, 4), ("*", V("ds", DW * b, DW * b + C + H), V("o_z", 0, 8)))
        cp(V("zf"), V("o_z"))
        quant(V("qz"), V("sz"), V("zt"))
        tt(V("de"), V("vb"), V("zf"), A_.subtract)
        ts(V("o_e"), V("de"), 4096.0, A_.mult)
        for b in range(4):
            mm(V("pd", 512 * b, 512 * b + K), V("wq", 128 * b, 128 * b + 128), V("wsc", 128 * b, 128 * b + 128), V("qz"), V("sz"))
            act(V("rsb", K * b, K * b + K), V("pd", 512 * b, 512 * b + K), ACT.Copy, scale=0.015625)
        if t == 0:
            act(V("srb"), ("*", V("lsb"), V("o_t", 0, 8)), ACT.Copy)
        if t == R - 1:
            ts(V("ef", 0, 8), V("de", 0, 8), 1024.0, A_.mult)
            tr(V("eft"), V("ef"))
            for k in range(8):
                dma("y", T.oe[k, :], T.eft[32 * (k // 2):32 * (k // 2) + 8, 16 * (k % 2):16 * (k % 2) + 16], [], [V("eft")])
        for h in range(2):
            tt(V("gt", 256 * h, 256 * h + 256), ("*", V("X"), V("o_e", 16 * h, 16 * h + 16)), V("rsb", 256 * h, 256 * h + 256), A_.add)
        cp(("*", V("X"), V("o_e")), V("gt"))
        if t + 1 < R:
            publish(t + 1)
        if t == 0:
            cp(V("qrb"), ("*", V("lqb"), V("o_t", 0, 8)))
            quant(V("qv"), V("sv"), V("vt"))
        if t == 1:
            ms(V("ef"), 0.0)

    qx, sx = V("qx%d" % R), V("sx%d" % R)
    quant(qx, sx, V("X"))
    mm(V("p0", 0, C), V("qv"), V("sv"), qx, sx)
    dma("y", T.oc[:], raw(qx), [], [qx])
    act(V("ys"), V("p0", 0, C), ACT.Copy)
    dma("s", T.y[:], T.ys[:], [], [V("ys")])
    for k in range(4):
        dma("s" if k % 2 else "y", T.osc[4 * k:4 * k + 4, :], T["sx%d" % R][32 * k:32 * k + 4, :], [], [sx])
    for sem, n in total.items():
        wait("g", (sem, n, {}))
